import numpy as np
import ml_dtypes


def mxq(x, axis, fmt="e4m3"):
    dtype, down = {"e4m3": (ml_dtypes.float8_e4m3fn, 7), "e5m2": (ml_dtypes.float8_e5m2, 14)}[fmt]
    v = np.moveaxis(np.asarray(x, np.float32).astype(ml_dtypes.bfloat16).astype(np.float64), axis, -1)
    blocks = v.reshape(v.shape[:-1] + (-1, 32))
    amax = np.abs(blocks).max(-1, keepdims=True)
    byte = np.maximum(np.where(amax > 0, np.frexp(amax)[1] - 1 + 127, 0) - down, 1)
    scale = np.exp2(byte - 127.0)
    codes = (blocks / scale).astype(np.float32).astype(dtype).astype(np.float64)
    return np.moveaxis((codes * scale).reshape(v.shape), -1, axis)


WIDE = False


def mx_kscale(k):
    if not WIDE:
        return np.ones(k)
    levels = np.array([10, -10, 5, -5, 0])
    if k % 512:
        return np.exp2(np.random.permutation(np.resize(levels, k // 32))).repeat(32)
    a = np.empty((k // 512, 16))
    for p in range(k // 512):
        a[p, :8] = np.random.permutation(np.resize(levels, 8))
        for g in range(8):
            far = levels[np.abs(levels - a[p, g]) >= 10]
            a[p, g + 8] = far[np.random.randint(len(far))]
    return np.exp2(a.ravel()).repeat(32)


def f64(x):
    return np.asarray(x).astype(np.float64)


def striped(idx):
    return np.tile(idx.reshape(-1, 16).T, (8, 1)).astype(np.uint16)


def unstriped(offs):
    return offs[:16].T.reshape(-1).astype(np.int64)


def striped8(idx):
    return np.concatenate([x.reshape(-1, 16).T for x in idx]).astype(np.uint16)


def runs(offs, k):
    lists = np.stack([offs[16 * r : 16 * r + 16].T.reshape(-1) for r in range(8)]).astype(np.int64)
    return lists[np.arange(k) % 512 // 64]


def pack_weight(w):
    k, n = w.shape
    w = f64(np.asarray(w, np.float32).astype(ml_dtypes.bfloat16)).reshape(k // 32, 32, n)
    amax = np.abs(w).max(1)
    byte = np.clip(np.where(amax > 0, np.frexp(amax)[1] - 1 + 127 - 7, 1), 1, 254)
    scaled = (w * np.exp2(127.0 - byte)[:, None, :]).reshape(k, n).astype(np.float32)
    words = np.ascontiguousarray(scaled.reshape(k // 512, 128, 4, n).transpose(0, 1, 3, 2)).astype(ml_dtypes.float8_e4m3fn).view(np.uint8)
    return words, np.ascontiguousarray(byte.astype(np.uint8).reshape(k // 512, 16, n))


def unpack_weight(words, scales):
    g, p, n, _ = words.shape
    vals = np.ascontiguousarray(words).view(ml_dtypes.float8_e4m3fn).astype(np.float64) * np.repeat(np.exp2(scales.astype(np.float64) - 127.0), 8, axis=1)[..., None]
    return vals.transpose(0, 1, 3, 2).reshape(g * 512, n)


K, T, S, H, G = 512, 1024, 512, 512, 2048


def setup_inputs():
    n = np.random.standard_normal
    s = mx_kscale(K)[:, None]
    packed_xT = pack_weight(n((K, T)) * s)
    packed_dT = pack_weight(n((K, G)) / s)
    return {
        "x_words": packed_xT[0],
        "x_scales": packed_xT[1],
        "w1": (n((K, H)) / np.sqrt(K) / s).astype(np.float32),
        "w2": (n((K, H)) / np.sqrt(K) / s).astype(np.float32),
        "tau": np.random.uniform(0.3, 0.9, (H, 1)).astype(np.float32),
        "gs": (np.random.uniform(0.5, 1.5, (K, 1)) * s).astype(np.float32),
        "d_words": packed_dT[0],
        "d_scales": packed_dT[1],
        "tau2": np.random.uniform(0.3, 0.9, (H, 1)).astype(np.float32),
        "offs": striped(np.random.permutation(T)[:S]),
        "two": striped(np.random.permutation(T)[:S]),
        "n1": striped8(np.stack([np.random.permutation(S) for _ in range(8)])),
        "n2": striped8(np.stack([np.random.permutation(S) for _ in range(8)])),
        "k1": striped8(np.random.randint(0, G, (8, H))),
        "n3": striped(np.random.permutation(S)),
    }


def reference(x_words, x_scales, w1, w2, tau, gs, d_words, d_scales, tau2, offs, two, n1, n2, k1, n3):
    d_k1 = unpack_weight(d_words, d_scales)[np.arange(K)[:, None], runs(k1, K)]
    x_two = unpack_weight(x_words, x_scales)[:, unstriped(two)]
    d = mxq(f64(w2), 0, "e4m3").T @ x_two
    top = d.max(axis=1, keepdims=True)
    ea = np.exp(f64(tau) * (d[np.arange(H)[:, None], runs(n1, H)] - top))
    xq = unpack_weight(x_words, x_scales)[:, unstriped(offs)]
    y = mxq(f64(w1), 0, "e4m3").T @ xq
    z = f64(gs) * ((2.0 * ea) * (y - (y[np.arange(H)[:, None], runs(n2, H)])) - (0.5 * d))
    h = 0.0625 * ((d_k1.T @ mxq(z, 0, "e4m3")))
    top2 = h.max(axis=1, keepdims=True)
    own = np.exp(f64(tau2) * (h - top2))
    ea2 = np.exp(f64(tau2) * (h[:, unstriped(n3)] - top2))
    return (2.0 * (h * own)) / (own + ea2 + 0.25)

@@ -1,0 +1,268 @@
+from contextlib import ExitStack
+
+import concourse.mybir as mybir
+
+K, T, S, H, G = 512, 1024, 512, 512, 2048
+FLOPS = 3 * 2 * K * H * S
+
+F32 = mybir.dt.float32
+BF16 = mybir.dt.bfloat16
+I32 = mybir.dt.int32
+U32 = mybir.dt.uint32
+U16 = mybir.dt.uint16
+U8 = mybir.dt.uint8
+FP8X4 = mybir.dt.float8_e4m3fn_x4
+ALU = mybir.AluOpType
+ACT = mybir.ActivationFunctionType
+
+P = 128
+PACK = 4
+TILES = H // P
+HALF = S // 2
+LIST_COLS = S // 16
+
+
+def tile_picked_twqpxbesh_none_p_kernel(
+    tc, x_words, x_scales, w1, w2, tau, gs, d_words, d_scales, tau2, offs, two, n1, n2, k1, n3, out
+):
+    nc = tc.nc
+    with ExitStack() as ctx:
+        lists = ctx.enter_context(tc.tile_pool(name="lists", bufs=1))
+        keep = ctx.enter_context(tc.tile_pool(name="keep", bufs=1))
+        psum = ctx.enter_context(tc.psum_pool(name="psum", bufs=1))
+
+        def list_tile(name, src):
+            tile = lists.tile([P, LIST_COLS], U16, name=name)
+            nc.sync.dma_start(tile[:], src)
+            return tile
+
+        def half_list(tile, hf):
+            return tile[:, hf * (LIST_COLS // 2) : (hf + 1) * (LIST_COLS // 2)]
+
+        def cols(hf):
+            return slice(hf * HALF, (hf + 1) * HALF)
+
+        def load_weight_half(name, w, hf):
+            raw = keep.tile([P, PACK, H // 2], F32, name=name)
+            nc.sync.dma_start(raw[:], w.rearrange("(p j) c -> p j c", j=PACK)[:, :, hf * (H // 2) : (hf + 1) * (H // 2)])
+            return raw
+
+        xs = keep.tile([P, T], U8, name="xs")
+        nc.vector.memset(xs[:].bitcast(I32), 0)
+        ds = keep.tile([P, G], U8, name="ds")
+        nc.gpsimd.memset(ds[:].bitcast(I32), 0)
+        dk_scales = keep.tile([P, H], U8, name="dk_scales", align_bytes=64)
+        nc.gpsimd.memset(dk_scales[:].bitcast(I32), 0)
+        sixteenth = keep.tile([P, 1], F32, name="sixteenth")
+        nc.gpsimd.memset(sixteenth[:], 0.0625)
+
+        two_l = list_tile("two_l", two)
+        xw = keep.tile([P, T], U32, name="xw")
+        nc.sync.dma_start(xw[:].bitcast(I32), x_words[0].rearrange("p n t -> p (n t)").bitcast(I32))
+        for q in range(4):
+            nc.sync.dma_start(xs[32 * q : 32 * q + 4, :].bitcast(I32), x_scales[0][4 * q : 4 * q + 4, :].bitcast(I32))
+        w2_raw = [load_weight_half("w2_raw%d" % hf, w2, hf) for hf in range(2)]
+        offs_l = list_tile("offs_l", offs)
+        w1_raw = [load_weight_half("w1_raw%d" % hf, w1, hf) for hf in range(2)]
+        n1_l = list_tile("n1_l", n1)
+        n2_l = list_tile("n2_l", n2)
+        k1_l = list_tile("k1_l", k1)
+        dw = keep.tile([P, G], U32, name="dw")
+        nc.sync.dma_start(dw[:].bitcast(I32), d_words[0].rearrange("p n t -> p (n t)").bitcast(I32))
+        n3_l = list_tile("n3_l", n3)
+
+        tau_t = keep.tile([P, TILES], F32, name="tau_t")
+        nc.gpsimd.dma_start(tau_t[:], tau.rearrange("(p t) o -> p (t o)", t=TILES))
+        gs_t = keep.tile([P, TILES], F32, name="gs_t")
+        nc.gpsimd.dma_start(gs_t[:], gs.rearrange("(p t) o -> p (t o)", t=TILES))
+        for r in range(2):
+            nc.gpsimd.dma_start(
+                ds[r:P:16, :].bitcast(I32), d_scales[0].rearrange("(g r) c -> r g c", r=2)[r].bitcast(I32)
+            )
+        tau2_t = keep.tile([P, TILES], F32, name="tau2_t")
+        with nc.allow_non_contiguous_dma(reason="one value a partition and tile"):
+            nc.gpsimd.dma_start(tau2_t[:], tau2.rearrange("(t p) o -> p (t o)", p=P))
+
+        gs_twice = keep.tile([P, TILES], F32, name="gs_twice")
+        nc.gpsimd.tensor_scalar(gs_twice[:], gs_t[:], 2.0, 0.0, ALU.mult, ALU.add)
+        gs_neg_half = keep.tile([P, TILES], F32, name="gs_neg_half")
+        nc.gpsimd.tensor_scalar(gs_neg_half[:], gs_t[:], -0.5, 0.0, ALU.mult, ALU.add)
+
+        def gather(name, window, offsets, dtype):
+            picked = keep.tile([P, S], dtype, name=name, align_bytes=64)
+            nc.vector.tensor_copy(picked[:], window[:].indirect(offsets[:]))
+            return picked
+
+        def round_weight(name, raws):
+            grouped = keep.tile([P, H * PACK], BF16, name=name, align_bytes=64)
+            dealt = grouped[:].rearrange("p (t m j) -> p m t j", t=TILES, j=PACK)
+            for hf in range(2):
+                nc.scalar.activation(
+                    dealt[:, hf * (P // 2) : (hf + 1) * (P // 2)],
+                    raws[hf][:].rearrange("p j (m t) -> p m t j", t=TILES),
+                    ACT.Copy,
+                )
+            return grouped
+
+        def quantize(codes, scales, values):
+            nc.vector.quantize_mx(out=codes.bitcast(FP8X4), scales=scales, in_=values)
+
+        def mx_tiles(name):
+            codes = keep.tile([P, H], U32, name=name + "_codes", align_bytes=64)
+            scales = keep.tile([P, H], U8, name=name + "_scales", align_bytes=64)
+            return codes, scales
+
+        def product(acc, lhs, lhs_cols, rhs, rhs_cols):
+            nc.tensor.matmul_mx(
+                out=acc,
+                lhsT=lhs[0][:, lhs_cols].bitcast(FP8X4),
+                lhsT_scale=lhs[1][:, lhs_cols],
+                rhs=rhs[0][:, rhs_cols].bitcast(FP8X4),
+                rhs_scale=rhs[1][:, rhs_cols],
+                start=True,
+                stop=True,
+            )
+
+        def rows(t):
+            return slice(t * P, (t + 1) * P)
+
+        x_two = (gather("x_two_words", xw, two_l, U32), gather("x_two_scales", xs, two_l, U8))
+        w2_grouped = round_weight("w2_grouped", w2_raw)
+        w1_grouped = round_weight("w1_grouped", w1_raw)
+        w2_q = mx_tiles("w2")
+        quantize(w2_q[0][:], w2_q[1][:], w2_grouped[:])
+        x_idx = (gather("x_idx_words", xw, offs_l, U32), gather("x_idx_scales", xs, offs_l, U8))
+
+        top = keep.tile([P, TILES], F32, name="top")
+        bias1 = keep.tile([P, TILES], F32, name="bias1")
+        d_sb = []
+        for t in range(TILES):
+            acc = psum.tile([P, S], F32, name="d_acc%d" % t, tag="bank%d" % t)
+            product(acc[:], w2_q, rows(t), x_two, slice(0, S))
+            window = keep.tile([P, S], F32, name="d_sb%d" % t)
+            nc.vector.tensor_scalar(window[:], acc[:], 1.0, None, ALU.mult, ALU.max, accum_out=top[:, t : t + 1])
+            nc.gpsimd.tensor_scalar(bias1[:, t : t + 1], top[:, t : t + 1], tau_t[:, t : t + 1], -1.0, ALU.mult, ALU.mult)
+            d_sb.append(window)
+
+        w1_q = mx_tiles("w1")
+        quantize(w1_q[0][:], w1_q[1][:], w1_grouped[:])
+        y_acc = []
+        for t in range(TILES):
+            acc = psum.tile([P, S], F32, name="y_acc%d" % t, tag="bank%d" % (TILES + t))
+            product(acc[:], w1_q, rows(t), x_idx, slice(0, S))
+            y_acc.append(acc)
+
+        ea = [keep.tile([P, TILES, HALF], F32, name="ea%d" % hf) for hf in range(2)]
+        y_far = [keep.tile([P, TILES, HALF], F32, name="y_far%d" % hf) for hf in range(2)]
+        diff = [keep.tile([P, TILES, HALF], F32, name="diff%d" % hf) for hf in range(2)]
+        prod = [keep.tile([P, TILES, HALF], F32, name="prod%d" % hf) for hf in range(2)]
+        z = [keep.tile([P, TILES, HALF], F32, name="z%d" % hf) for hf in range(2)]
+        y_sb = [keep.tile([P, S], F32, name="y_sb%d" % t) for t in range(TILES)]
+
+        def fetch_ea(t, hf):
+            nc.scalar.activation(
+                ea[hf][:, t, :], d_sb[t][:].indirect(half_list(n1_l, hf)), ACT.Exp,
+                bias=bias1[:, t : t + 1], scale=tau_t[:, t : t + 1],
+            )
+
+        def fetch_y(t, hf):
+            nc.scalar.activation(y_far[hf][:, t, :], y_sb[t][:].indirect(half_list(n2_l, hf)), ACT.Copy)
+
+        def difference(t, hf):
+            nc.vector.scalar_tensor_tensor(
+                diff[hf][:, t, :], y_acc[t][:, cols(hf)], gs_twice[:, t : t + 1], y_far[hf][:, t, :], ALU.mult, ALU.subtract
+            )
+
+        def multiply(t, hf):
+            nc.vector.tensor_tensor(prod[hf][:, t, :], ea[hf][:, t, :], diff[hf][:, t, :], ALU.mult)
+
+        def finish_z(t, hf):
+            nc.vector.scalar_tensor_tensor(
+                z[hf][:, t, :], d_sb[t][:, cols(hf)], gs_neg_half[:, t : t + 1], prod[hf][:, t, :], ALU.mult, ALU.add
+            )
+
+        z_q = mx_tiles("z")
+
+        def quantize_z(hf):
+            grouped = keep.tile([P, HALF * PACK], BF16, name="z_grouped%d" % hf, align_bytes=64)
+            nc.vector.tensor_copy(
+                grouped[:].rearrange("p (c i t) -> p c t i", i=4, t=PACK),
+                z[hf][:].rearrange("p t (c i) -> p c t i", i=4),
+            )
+            quantize(z_q[0][:, cols(hf)], z_q[1][:, cols(hf)], grouped[:])
+
+        for t in range(TILES):
+            fetch_ea(t, 0)
+        for t in range(TILES):
+            nc.scalar.activation(y_sb[t][:], y_acc[t][:], ACT.Copy, scale=gs_twice[:, t : t + 1])
+            fetch_y(t, 0)
+
+        dk_words = gather("dk_words", dw, k1_l, U32)
+        dk_picked = gather("dk_picked", ds, k1_l, U8)
+        for r in range(4):
+            src = 16 * (r // 2) + r % 2
+            nc.sync.dma_start(dk_scales[r:P:32, :].bitcast(I32), dk_picked[src:P:32, :].bitcast(I32))
+        dk = (dk_words, dk_scales)
+
+        h_acc = [psum.tile([P, S], F32, name="h_acc%d" % t, tag="bank%d" % t) for t in range(TILES)]
+        h_sb = [keep.tile([P, S], F32, name="h_sb%d" % t, tag="h_sb%d" % t) for t in range(TILES)]
+        top2_half = keep.tile([P, TILES], F32, name="top2_half")
+        top2 = keep.tile([P, TILES], F32, name="top2")
+        bias2 = keep.tile([P, TILES], F32, name="bias2")
+
+        for t in range(TILES):
+            difference(t, 0)
+            if t > 0:
+                finish_z(t - 1, 0)
+            multiply(t, 0)
+        finish_z(TILES - 1, 0)
+        for t in range(TILES):
+            fetch_y(t, 1)
+        for t in range(TILES):
+            fetch_ea(t, 1)
+        for t in range(TILES):
+            difference(t, 1)
+        quantize_z(0)
+        for t in range(TILES):
+            product(h_acc[t][:, cols(0)], dk, rows(t), z_q, cols(0))
+        for t in range(TILES):
+            multiply(t, 1)
+            if t > 0:
+                finish_z(t - 1, 1)
+            nc.vector.tensor_scalar(
+                h_sb[t][:, cols(0)], h_acc[t][:, cols(0)], 0.0625, None, ALU.mult, ALU.max, accum_out=top2_half[:, t : t + 1]
+            )
+        finish_z(TILES - 1, 1)
+        quantize_z(1)
+        for t in range(TILES):
+            product(h_acc[t][:, cols(1)], dk, rows(t), z_q, cols(1))
+
+        own = [keep.tile([P, S], F32, name="own%d" % t) for t in range(TILES)]
+        ea2 = [keep.tile([P, S], F32, name="ea2_%d" % t) for t in range(TILES)]
+        num = [keep.tile([P, S], F32, name="num%d" % t) for t in range(TILES)]
+        both = [keep.tile([P, S], F32, name="both%d" % t) for t in range(TILES)]
+        square = [keep.tile([P, S], F32, name="square%d" % t, tag="square%d" % t) for t in range(TILES)]
+        for t in range(TILES):
+            nc.vector.tensor_scalar(
+                h_sb[t][:, cols(1)], h_acc[t][:, cols(1)], 0.0625, top2_half[:, t : t + 1], ALU.mult, ALU.max,
+                accum_out=top2[:, t : t + 1],
+            )
+            nc.gpsimd.tensor_scalar(bias2[:, t : t + 1], top2[:, t : t + 1], tau2_t[:, t : t + 1], -1.0, ALU.mult, ALU.mult)
+        for t in range(TILES):
+            nc.scalar.activation(own[t][:], h_sb[t][:], ACT.Exp, bias=bias2[:, t : t + 1], scale=tau2_t[:, t : t + 1])
+            for hf in range(2):
+                nc.scalar.activation(
+                    ea2[t][:, cols(hf)], h_sb[t][:].indirect(half_list(n3_l, hf)), ACT.Exp,
+                    bias=bias2[:, t : t + 1], scale=tau2_t[:, t : t + 1],
+                )
+            nc.vector.scalar_tensor_tensor(num[t][:], h_acc[t][:], 0.125, own[t][:], ALU.mult, ALU.mult)
+            nc.vector.tensor_tensor(both[t][:], own[t][:], ea2[t][:], ALU.add)
+            nc.vector.scalar_tensor_tensor(square[t][:], both[t][:], 0.5, both[t][:], ALU.add, ALU.mult)
+
+        for t in range(TILES):
+            tag = "h_sb%d" % (TILES - 1) if t == 0 else "square%d" % (t - 1)
+            inverse = keep.tile([P, S], F32, name="inverse%d" % t, tag=tag)
+            nc.scalar.activation(inverse[:], square[t][:], ACT.Abs_reciprocal_sqrt, bias=sixteenth[:], scale=1.0)
+            result = keep.tile([P, S], F32, name="result%d" % t)
+            nc.vector.tensor_tensor(result[:], num[t][:], inverse[:], ALU.mult)
+            nc.sync.dma_start(out[rows(t), :], result[:])

@@ -48,28 +48,31 @@ def tile_picked_twqpxbesh_none_p_kernel(
             return raw
 
         xs = keep.tile([P, T], U8, name="xs")
-        nc.vector.memset(xs[:].bitcast(I32), 0)
+        nc.gpsimd.memset(xs[:].bitcast(I32), 0)
         ds = keep.tile([P, G], U8, name="ds")
         nc.gpsimd.memset(ds[:].bitcast(I32), 0)
         dk_scales = keep.tile([P, H], U8, name="dk_scales", align_bytes=64)
         nc.gpsimd.memset(dk_scales[:].bitcast(I32), 0)
-        sixteenth = keep.tile([P, 1], F32, name="sixteenth")
-        nc.gpsimd.memset(sixteenth[:], 0.0625)
 
-        two_l = list_tile("two_l", two)
+        offs_l = list_tile("offs_l", offs)
         xw = keep.tile([P, T], U32, name="xw")
         nc.sync.dma_start(xw[:].bitcast(I32), x_words[0].rearrange("p n t -> p (n t)").bitcast(I32))
         for q in range(4):
             nc.sync.dma_start(xs[32 * q : 32 * q + 4, :].bitcast(I32), x_scales[0][4 * q : 4 * q + 4, :].bitcast(I32))
-        w2_raw = [load_weight_half("w2_raw%d" % hf, w2, hf) for hf in range(2)]
-        offs_l = list_tile("offs_l", offs)
         w1_raw = [load_weight_half("w1_raw%d" % hf, w1, hf) for hf in range(2)]
-        n1_l = list_tile("n1_l", n1)
-        n2_l = list_tile("n2_l", n2)
+        w2_raw = [load_weight_half("w2_raw0", w2, 0)]
+        two_l = list_tile("two_l", two)
+        w2_raw.append(load_weight_half("w2_raw1", w2, 1))
         k1_l = list_tile("k1_l", k1)
+        n2_l = list_tile("n2_l", n2)
+        n1_l = list_tile("n1_l", n1)
         dw = keep.tile([P, G], U32, name="dw")
         nc.sync.dma_start(dw[:].bitcast(I32), d_words[0].rearrange("p n t -> p (n t)").bitcast(I32))
         n3_l = list_tile("n3_l", n3)
+
+        tau2_t = keep.tile([P, TILES], F32, name="tau2_t")
+        with nc.allow_non_contiguous_dma(reason="one value a partition and tile"):
+            nc.sync.dma_start(tau2_t[:], tau2.rearrange("(t p) o -> p (t o)", p=P))
 
         tau_t = keep.tile([P, TILES], F32, name="tau_t")
         nc.gpsimd.dma_start(tau_t[:], tau.rearrange("(p t) o -> p (t o)", t=TILES))
@@ -79,29 +82,28 @@ def tile_picked_twqpxbesh_none_p_kernel(
             nc.gpsimd.dma_start(
                 ds[r:P:16, :].bitcast(I32), d_scales[0].rearrange("(g r) c -> r g c", r=2)[r].bitcast(I32)
             )
-        tau2_t = keep.tile([P, TILES], F32, name="tau2_t")
-        with nc.allow_non_contiguous_dma(reason="one value a partition and tile"):
-            nc.gpsimd.dma_start(tau2_t[:], tau2.rearrange("(t p) o -> p (t o)", p=P))
-
         gs_twice = keep.tile([P, TILES], F32, name="gs_twice")
         nc.gpsimd.tensor_scalar(gs_twice[:], gs_t[:], 2.0, 0.0, ALU.mult, ALU.add)
         gs_neg_half = keep.tile([P, TILES], F32, name="gs_neg_half")
         nc.gpsimd.tensor_scalar(gs_neg_half[:], gs_t[:], -0.5, 0.0, ALU.mult, ALU.add)
 
-        def gather(name, window, offsets, dtype):
-            picked = keep.tile([P, S], dtype, name=name, align_bytes=64)
+        def gather(name, window, offsets, dtype, tag=None):
+            picked = keep.tile([P, S], dtype, name=name, tag=tag or name, align_bytes=64)
             nc.vector.tensor_copy(picked[:], window[:].indirect(offsets[:]))
             return picked
 
-        def round_weight(name, raws):
-            grouped = keep.tile([P, H * PACK], BF16, name=name, align_bytes=64)
+        def round_weight(name, raws, engines):
+            grouped = keep.tile([P, H * PACK], BF16, name=name, tag=name, align_bytes=64)
             dealt = grouped[:].rearrange("p (t m j) -> p m t j", t=TILES, j=PACK)
             for hf in range(2):
-                nc.scalar.activation(
-                    dealt[:, hf * (P // 2) : (hf + 1) * (P // 2)],
-                    raws[hf][:].rearrange("p j (m t) -> p m t j", t=TILES),
-                    ACT.Copy,
-                )
+                dst = dealt[:, hf * (P // 2) : (hf + 1) * (P // 2)]
+                src = raws[hf][:].rearrange("p j (m t) -> p m t j", t=TILES)
+                if engines[hf] == "vector":
+                    nc.vector.tensor_copy(dst, src)
+                elif engines[hf] == "gpsimd":
+                    nc.gpsimd.tensor_copy(dst, src)
+                else:
+                    nc.scalar.activation(dst, src, ACT.Copy)
             return grouped
 
         def quantize(codes, scales, values):
@@ -126,24 +128,9 @@ def tile_picked_twqpxbesh_none_p_kernel(
         def rows(t):
             return slice(t * P, (t + 1) * P)
 
-        x_two = (gather("x_two_words", xw, two_l, U32), gather("x_two_scales", xs, two_l, U8))
-        w2_grouped = round_weight("w2_grouped", w2_raw)
-        w1_grouped = round_weight("w1_grouped", w1_raw)
-        w2_q = mx_tiles("w2")
-        quantize(w2_q[0][:], w2_q[1][:], w2_grouped[:])
         x_idx = (gather("x_idx_words", xw, offs_l, U32), gather("x_idx_scales", xs, offs_l, U8))
-
-        top = keep.tile([P, TILES], F32, name="top")
-        bias1 = keep.tile([P, TILES], F32, name="bias1")
-        d_sb = []
-        for t in range(TILES):
-            acc = psum.tile([P, S], F32, name="d_acc%d" % t, tag="bank%d" % t)
-            product(acc[:], w2_q, rows(t), x_two, slice(0, S))
-            window = keep.tile([P, S], F32, name="d_sb%d" % t)
-            nc.vector.tensor_scalar(window[:], acc[:], 1.0, None, ALU.mult, ALU.max, accum_out=top[:, t : t + 1])
-            nc.gpsimd.tensor_scalar(bias1[:, t : t + 1], top[:, t : t + 1], tau_t[:, t : t + 1], -1.0, ALU.mult, ALU.mult)
-            d_sb.append(window)
-
+        w1_grouped = round_weight("w1_grouped", w1_raw, ("scalar", "vector"))
+        w2_grouped = round_weight("w2_grouped", w2_raw, ("scalar", "gpsimd"))
         w1_q = mx_tiles("w1")
         quantize(w1_q[0][:], w1_q[1][:], w1_grouped[:])
         y_acc = []
@@ -151,117 +138,122 @@ def tile_picked_twqpxbesh_none_p_kernel(
             acc = psum.tile([P, S], F32, name="y_acc%d" % t, tag="bank%d" % (TILES + t))
             product(acc[:], w1_q, rows(t), x_idx, slice(0, S))
             y_acc.append(acc)
+        x_two = (gather("x_two_words", xw, two_l, U32), gather("x_two_scales", xs, two_l, U8))
+        w2_q = mx_tiles("w2")
+        quantize(w2_q[0][:], w2_q[1][:], w2_grouped[:])
 
-        ea = [keep.tile([P, TILES, HALF], F32, name="ea%d" % hf) for hf in range(2)]
-        y_far = [keep.tile([P, TILES, HALF], F32, name="y_far%d" % hf) for hf in range(2)]
-        diff = [keep.tile([P, TILES, HALF], F32, name="diff%d" % hf) for hf in range(2)]
-        prod = [keep.tile([P, TILES, HALF], F32, name="prod%d" % hf) for hf in range(2)]
-        z = [keep.tile([P, TILES, HALF], F32, name="z%d" % hf) for hf in range(2)]
-        y_sb = [keep.tile([P, S], F32, name="y_sb%d" % t) for t in range(TILES)]
+        dk_picked = gather("dk_picked", ds, k1_l, U8, tag="w2_grouped")
 
-        def fetch_ea(t, hf):
+        ea = keep.tile([P, TILES, S], F32, name="ea")
+        y_far = keep.tile([P, TILES, S], F32, name="y_far")
+        work = keep.tile([P, TILES - 1, S], F32, name="work")
+        z = keep.tile([P, TILES, S], F32, name="z")
+
+        top = keep.tile([P, TILES], F32, name="top")
+        bias1 = keep.tile([P, TILES], F32, name="bias1")
+        d_sb = []
+        d_acc = []
+        for t in range(TILES):
+            acc = psum.tile([P, S], F32, name="d_acc%d" % t, tag="bank%d" % t)
+            product(acc[:], w2_q, rows(t), x_two, slice(0, S))
+            window = keep.tile([P, 2 * S], F32, name="d_sb%d" % t, tag="d_sb%d" % t)
+            nc.vector.tensor_scalar(window[:, :S], acc[:], 1.0, None, ALU.mult, ALU.max, accum_out=top[:, t : t + 1])
+            nc.gpsimd.tensor_scalar(bias1[:, t : t + 1], top[:, t : t + 1], tau_t[:, t : t + 1], -1.0, ALU.mult, ALU.mult)
+            d_sb.append(window)
+            d_acc.append(acc)
+
+        last = TILES - 1
+
+        def fetch_ea(t, span, offsets):
             nc.scalar.activation(
-                ea[hf][:, t, :], d_sb[t][:].indirect(half_list(n1_l, hf)), ACT.Exp,
-                bias=bias1[:, t : t + 1], scale=tau_t[:, t : t + 1],
+                ea[:, t, span], d_sb[t][:].indirect(offsets), ACT.Exp, bias=bias1[:, t : t + 1], scale=tau_t[:, t : t + 1]
             )
-
-        def fetch_y(t, hf):
-            nc.scalar.activation(y_far[hf][:, t, :], y_sb[t][:].indirect(half_list(n2_l, hf)), ACT.Copy)
-
-        def difference(t, hf):
-            nc.vector.scalar_tensor_tensor(
-                diff[hf][:, t, :], y_acc[t][:, cols(hf)], gs_twice[:, t : t + 1], y_far[hf][:, t, :], ALU.mult, ALU.subtract
-            )
-
-        def multiply(t, hf):
-            nc.vector.tensor_tensor(prod[hf][:, t, :], ea[hf][:, t, :], diff[hf][:, t, :], ALU.mult)
-
-        def finish_z(t, hf):
-            nc.vector.scalar_tensor_tensor(
-                z[hf][:, t, :], d_sb[t][:, cols(hf)], gs_neg_half[:, t : t + 1], prod[hf][:, t, :], ALU.mult, ALU.add
-            )
-
-        z_q = mx_tiles("z")
-
-        def quantize_z(hf):
-            grouped = keep.tile([P, HALF * PACK], BF16, name="z_grouped%d" % hf, align_bytes=64)
-            nc.vector.tensor_copy(
-                grouped[:].rearrange("p (c i t) -> p c t i", i=4, t=PACK),
-                z[hf][:].rearrange("p t (c i) -> p c t i", i=4),
-            )
-            quantize(z_q[0][:, cols(hf)], z_q[1][:, cols(hf)], grouped[:])
 
         for t in range(TILES):
-            fetch_ea(t, 0)
-        for t in range(TILES):
-            nc.scalar.activation(y_sb[t][:], y_acc[t][:], ACT.Copy, scale=gs_twice[:, t : t + 1])
-            fetch_y(t, 0)
+            y_sb = keep.tile([P, 2 * S], F32, name="y_sb%d" % t, tag="y_sb%d" % t if t < last else "d_sb0")
+            nc.scalar.activation(y_sb[:, :S], y_acc[t][:], ACT.Copy, scale=gs_twice[:, t : t + 1])
+            nc.scalar.activation(y_far[:, t, :], y_sb[:].indirect(n2_l[:]), ACT.Copy)
+            if t < last:
+                fetch_ea(t, slice(0, S), n1_l[:])
+        for hf in range(2):
+            fetch_ea(last, cols(hf), half_list(n1_l, hf))
 
+        def difference(t):
+            nc.vector.scalar_tensor_tensor(
+                work[:, min(t, last - 1), :], y_acc[t][:], gs_twice[:, t : t + 1], y_far[:, t, :], ALU.mult, ALU.subtract
+            )
+
+        for t in range(last):
+            difference(t)
         dk_words = gather("dk_words", dw, k1_l, U32)
-        dk_picked = gather("dk_picked", ds, k1_l, U8)
         for r in range(4):
             src = 16 * (r // 2) + r % 2
             nc.sync.dma_start(dk_scales[r:P:32, :].bitcast(I32), dk_picked[src:P:32, :].bitcast(I32))
         dk = (dk_words, dk_scales)
 
-        h_acc = [psum.tile([P, S], F32, name="h_acc%d" % t, tag="bank%d" % t) for t in range(TILES)]
-        h_sb = [keep.tile([P, S], F32, name="h_sb%d" % t, tag="h_sb%d" % t) for t in range(TILES)]
-        top2_half = keep.tile([P, TILES], F32, name="top2_half")
+        def multiply(engine, t, span):
+            slot = work[:, min(t, last - 1), span]
+            engine.tensor_tensor(slot, ea[:, t, span], slot, ALU.mult)
+
+        def finish_z(t, span):
+            nc.vector.scalar_tensor_tensor(
+                z[:, t, span], d_acc[t][:, span], gs_neg_half[:, t : t + 1], work[:, min(t, last - 1), span], ALU.mult, ALU.add
+            )
+
+        for t in range(last):
+            multiply(nc.gpsimd, t, slice(0, S))
+            finish_z(t, slice(0, S))
+        difference(last)
+        multiply(nc.vector, last, cols(0))
+        multiply(nc.vector, last, cols(1))
+        finish_z(last, cols(0))
+
+        z_q = mx_tiles("z")
+        z_grouped = [keep.tile([P, HALF * PACK], BF16, name="z_grouped%d" % hf, align_bytes=64) for hf in range(2)]
+
+        def weave(hf):
+            return (
+                z_grouped[hf][:].rearrange("p (c i t) -> p c t i", i=4, t=PACK),
+                z[:, :, cols(hf)].rearrange("p t (c i) -> p c t i", i=4),
+            )
+
+        finish_z(last, cols(1))
+        nc.scalar.activation(*weave(0), ACT.Copy)
+        nc.vector.tensor_copy(*weave(1))
+
+        h_acc = [psum.tile([P, S], F32, name="h_acc%d" % t, tag="bank%d" % (TILES + t)) for t in range(TILES)]
+        h_sb = [keep.tile([P, 2 * S], F32, name="h_sb%d" % t, tag="h_sb%d" % t) for t in range(TILES)]
         top2 = keep.tile([P, TILES], F32, name="top2")
         bias2 = keep.tile([P, TILES], F32, name="bias2")
-
+        for hf in range(2):
+            quantize(z_q[0][:, cols(hf)], z_q[1][:, cols(hf)], z_grouped[hf][:])
         for t in range(TILES):
-            difference(t, 0)
-            if t > 0:
-                finish_z(t - 1, 0)
-            multiply(t, 0)
-        finish_z(TILES - 1, 0)
-        for t in range(TILES):
-            fetch_y(t, 1)
-        for t in range(TILES):
-            fetch_ea(t, 1)
-        for t in range(TILES):
-            difference(t, 1)
-        quantize_z(0)
-        for t in range(TILES):
-            product(h_acc[t][:, cols(0)], dk, rows(t), z_q, cols(0))
-        for t in range(TILES):
-            multiply(t, 1)
-            if t > 0:
-                finish_z(t - 1, 1)
-            nc.vector.tensor_scalar(
-                h_sb[t][:, cols(0)], h_acc[t][:, cols(0)], 0.0625, None, ALU.mult, ALU.max, accum_out=top2_half[:, t : t + 1]
-            )
-        finish_z(TILES - 1, 1)
-        quantize_z(1)
-        for t in range(TILES):
-            product(h_acc[t][:, cols(1)], dk, rows(t), z_q, cols(1))
+            for hf in range(2):
+                product(h_acc[t][:, cols(hf)], dk, rows(t), z_q, cols(hf))
 
         own = [keep.tile([P, S], F32, name="own%d" % t) for t in range(TILES)]
         ea2 = [keep.tile([P, S], F32, name="ea2_%d" % t) for t in range(TILES)]
         num = [keep.tile([P, S], F32, name="num%d" % t) for t in range(TILES)]
         both = [keep.tile([P, S], F32, name="both%d" % t) for t in range(TILES)]
-        square = [keep.tile([P, S], F32, name="square%d" % t, tag="square%d" % t) for t in range(TILES)]
+        square = [keep.tile([P, S], F32, name="square%d" % t) for t in range(TILES)]
         for t in range(TILES):
             nc.vector.tensor_scalar(
-                h_sb[t][:, cols(1)], h_acc[t][:, cols(1)], 0.0625, top2_half[:, t : t + 1], ALU.mult, ALU.max,
-                accum_out=top2[:, t : t + 1],
+                h_sb[t][:, :S], h_acc[t][:], 0.0625, None, ALU.mult, ALU.max, accum_out=top2[:, t : t + 1]
             )
             nc.gpsimd.tensor_scalar(bias2[:, t : t + 1], top2[:, t : t + 1], tau2_t[:, t : t + 1], -1.0, ALU.mult, ALU.mult)
         for t in range(TILES):
-            nc.scalar.activation(own[t][:], h_sb[t][:], ACT.Exp, bias=bias2[:, t : t + 1], scale=tau2_t[:, t : t + 1])
-            for hf in range(2):
-                nc.scalar.activation(
-                    ea2[t][:, cols(hf)], h_sb[t][:].indirect(half_list(n3_l, hf)), ACT.Exp,
-                    bias=bias2[:, t : t + 1], scale=tau2_t[:, t : t + 1],
-                )
+            nc.scalar.activation(own[t][:], h_sb[t][:, :S], ACT.Exp, bias=bias2[:, t : t + 1], scale=tau2_t[:, t : t + 1])
+            nc.scalar.activation(
+                ea2[t][:], h_sb[t][:].indirect(n3_l[:]), ACT.Exp, bias=bias2[:, t : t + 1], scale=tau2_t[:, t : t + 1]
+            )
             nc.vector.scalar_tensor_tensor(num[t][:], h_acc[t][:], 0.125, own[t][:], ALU.mult, ALU.mult)
             nc.vector.tensor_tensor(both[t][:], own[t][:], ea2[t][:], ALU.add)
             nc.vector.scalar_tensor_tensor(square[t][:], both[t][:], 0.5, both[t][:], ALU.add, ALU.mult)
 
+        sixteenth = keep.tile([P, 1], F32, name="sixteenth", tag="h_sb%d" % last)
+        nc.gpsimd.memset(sixteenth[:], 0.0625)
         for t in range(TILES):
-            tag = "h_sb%d" % (TILES - 1) if t == 0 else "square%d" % (t - 1)
-            inverse = keep.tile([P, S], F32, name="inverse%d" % t, tag=tag)
+            inverse = keep.tile([P, S], F32, name="inverse%d" % t)
             nc.scalar.activation(inverse[:], square[t][:], ACT.Abs_reciprocal_sqrt, bias=sixteenth[:], scale=1.0)
             result = keep.tile([P, S], F32, name="result%d" % t)
             nc.vector.tensor_tensor(result[:], num[t][:], inverse[:], ALU.mult)

@@ -84,6 +84,8 @@ def tile_picked_twqpxbesh_none_p_kernel(
             )
         gs_twice = keep.tile([P, TILES], F32, name="gs_twice")
         nc.gpsimd.tensor_scalar(gs_twice[:], gs_t[:], 2.0, 0.0, ALU.mult, ALU.add)
+        tau_neg = keep.tile([P, TILES], F32, name="tau_neg")
+        nc.gpsimd.tensor_scalar(tau_neg[:], tau_t[:], -1.0, 0.0, ALU.mult, ALU.add)
         gs_neg_half = keep.tile([P, TILES], F32, name="gs_neg_half")
         nc.gpsimd.tensor_scalar(gs_neg_half[:], gs_t[:], -0.5, 0.0, ALU.mult, ALU.add)
 
@@ -110,8 +112,14 @@ def tile_picked_twqpxbesh_none_p_kernel(
             nc.vector.quantize_mx(out=codes.bitcast(FP8X4), scales=scales, in_=values)
 
         def mx_tiles(name):
-            codes = keep.tile([P, H], U32, name=name + "_codes", align_bytes=64)
-            scales = keep.tile([P, H], U8, name=name + "_scales", align_bytes=64)
+            codes = keep.tile([P, H], U32, name=name + "_codes", tag=name + "_codes", align_bytes=64)
+            scales = keep.tile([P, H], U8, name=name + "_scales", tag=name + "_scales", align_bytes=64)
+            return codes, scales
+
+        def quantize_weight(name, grouped):
+            codes, scales = mx_tiles(name)
+            quantize(codes[:, :P], scales[:, :P], grouped[:, : P * PACK])
+            quantize(codes[:, P:], scales[:, P:], grouped[:, P * PACK :])
             return codes, scales
 
         def product(acc, lhs, lhs_cols, rhs, rhs_cols):
@@ -131,26 +139,22 @@ def tile_picked_twqpxbesh_none_p_kernel(
         x_idx = (gather("x_idx_words", xw, offs_l, U32), gather("x_idx_scales", xs, offs_l, U8))
         w1_grouped = round_weight("w1_grouped", w1_raw, ("scalar", "vector"))
         w2_grouped = round_weight("w2_grouped", w2_raw, ("scalar", "gpsimd"))
-        w1_q = mx_tiles("w1")
-        quantize(w1_q[0][:], w1_q[1][:], w1_grouped[:])
+        w1_q = quantize_weight("w1", w1_grouped)
         y_acc = []
         for t in range(TILES):
             acc = psum.tile([P, S], F32, name="y_acc%d" % t, tag="bank%d" % (TILES + t))
             product(acc[:], w1_q, rows(t), x_idx, slice(0, S))
             y_acc.append(acc)
         x_two = (gather("x_two_words", xw, two_l, U32), gather("x_two_scales", xs, two_l, U8))
-        w2_q = mx_tiles("w2")
-        quantize(w2_q[0][:], w2_q[1][:], w2_grouped[:])
+        w2_q = quantize_weight("w2", w2_grouped)
 
-        dk_picked = gather("dk_picked", ds, k1_l, U8, tag="w2_grouped")
-
-        ea = keep.tile([P, TILES, S], F32, name="ea")
         y_far = keep.tile([P, TILES, S], F32, name="y_far")
-        work = keep.tile([P, TILES - 1, S], F32, name="work")
+        diff = keep.tile([P, 2, S], F32, name="diff")
+        prod = keep.tile([P, 2, S], F32, name="prod")
         z = keep.tile([P, TILES, S], F32, name="z")
 
         top = keep.tile([P, TILES], F32, name="top")
-        bias1 = keep.tile([P, TILES], F32, name="bias1")
+        bias1 = [keep.tile([P, 1], F32, name="bias1_%d" % t) for t in range(TILES)]
         d_sb = []
         d_acc = []
         for t in range(TILES):
@@ -158,68 +162,90 @@ def tile_picked_twqpxbesh_none_p_kernel(
             product(acc[:], w2_q, rows(t), x_two, slice(0, S))
             window = keep.tile([P, 2 * S], F32, name="d_sb%d" % t, tag="d_sb%d" % t)
             nc.vector.tensor_scalar(window[:, :S], acc[:], 1.0, None, ALU.mult, ALU.max, accum_out=top[:, t : t + 1])
-            nc.gpsimd.tensor_scalar(bias1[:, t : t + 1], top[:, t : t + 1], tau_t[:, t : t + 1], -1.0, ALU.mult, ALU.mult)
+            if t < 2:
+                nc.scalar.activation(bias1[t][:], top[:, t : t + 1], ACT.Copy, scale=tau_neg[:, t : t + 1])
+            else:
+                nc.gpsimd.tensor_tensor(bias1[t][:], top[:, t : t + 1], tau_neg[:, t : t + 1], ALU.mult)
             d_sb.append(window)
             d_acc.append(acc)
 
         last = TILES - 1
 
+        y_sb = []
+
+        def ea(t, span):
+            return y_sb[t][:, S + span.start : S + span.stop]
+
+        def diff_of(t, span):
+            return ea(1, span) if t == last else diff[:, min(t, 1), span]
+
+        def difference(t):
+            nc.gpsimd.tensor_tensor(diff_of(t, slice(0, S)), y_sb[t][:, :S], y_far[:, t, :], ALU.subtract)
+
         def fetch_ea(t, span, offsets):
             nc.scalar.activation(
-                ea[:, t, span], d_sb[t][:].indirect(offsets), ACT.Exp, bias=bias1[:, t : t + 1], scale=tau_t[:, t : t + 1]
+                ea(t, span), d_sb[t][:].indirect(offsets), ACT.Exp, bias=bias1[t][:], scale=tau_t[:, t : t + 1]
             )
 
         for t in range(TILES):
-            y_sb = keep.tile([P, 2 * S], F32, name="y_sb%d" % t, tag="y_sb%d" % t if t < last else "d_sb0")
-            nc.scalar.activation(y_sb[:, :S], y_acc[t][:], ACT.Copy, scale=gs_twice[:, t : t + 1])
-            nc.scalar.activation(y_far[:, t, :], y_sb[:].indirect(n2_l[:]), ACT.Copy)
+            if t < 2:
+                window = keep.tile([P, 2 * S], F32, name="y_sb%d" % t)
+                nc.scalar.activation(window[:, :S], y_acc[t][:], ACT.Copy, scale=gs_twice[:, t : t + 1])
+            else:
+                window = keep.tile([P, 2 * S], F32, name="y_sb%d" % t, tag=("w2_codes", "w2_scales")[t - 2], align_bytes=64)
+                nc.vector.tensor_scalar(window[:, :S], y_acc[t][:], gs_twice[:, t : t + 1], None, ALU.mult)
+            y_sb.append(window)
+            nc.scalar.activation(y_far[:, t, :], window[:].indirect(n2_l[:]), ACT.Copy)
+            if t < 2:
+                difference(t)
             if t < last:
                 fetch_ea(t, slice(0, S), n1_l[:])
         for hf in range(2):
             fetch_ea(last, cols(hf), half_list(n1_l, hf))
 
-        def difference(t):
-            nc.vector.scalar_tensor_tensor(
-                work[:, min(t, last - 1), :], y_acc[t][:], gs_twice[:, t : t + 1], y_far[:, t, :], ALU.mult, ALU.subtract
-            )
-
-        for t in range(last):
-            difference(t)
+        dk_picked = gather("dk_picked", ds, k1_l, U8, tag="x_two_words")
         dk_words = gather("dk_words", dw, k1_l, U32)
         for r in range(4):
             src = 16 * (r // 2) + r % 2
             nc.sync.dma_start(dk_scales[r:P:32, :].bitcast(I32), dk_picked[src:P:32, :].bitcast(I32))
         dk = (dk_words, dk_scales)
 
+        slots = (0, 1, 1, 0)
+
         def multiply(engine, t, span):
-            slot = work[:, min(t, last - 1), span]
-            engine.tensor_tensor(slot, ea[:, t, span], slot, ALU.mult)
+            engine.tensor_tensor(prod[:, slots[t], span], ea(t, span), diff_of(t, span), ALU.mult)
 
         def finish_z(t, span):
             nc.vector.scalar_tensor_tensor(
-                z[:, t, span], d_acc[t][:, span], gs_neg_half[:, t : t + 1], work[:, min(t, last - 1), span], ALU.mult, ALU.add
+                z[:, t, span], d_acc[t][:, span], gs_neg_half[:, t : t + 1], prod[:, slots[t], span], ALU.mult, ALU.add
             )
 
-        for t in range(last):
+        for t in range(2):
             multiply(nc.gpsimd, t, slice(0, S))
             finish_z(t, slice(0, S))
+        difference(2)
         difference(last)
+        multiply(nc.vector, 2, slice(0, S))
         multiply(nc.vector, last, cols(0))
+        finish_z(2, slice(0, S))
         multiply(nc.vector, last, cols(1))
         finish_z(last, cols(0))
 
         z_q = mx_tiles("z")
         z_grouped = [keep.tile([P, HALF * PACK], BF16, name="z_grouped%d" % hf, align_bytes=64) for hf in range(2)]
 
-        def weave(hf):
+        def weave(hf, first, count):
+            start = hf * HALF + first
             return (
-                z_grouped[hf][:].rearrange("p (c i t) -> p c t i", i=4, t=PACK),
-                z[:, :, cols(hf)].rearrange("p t (c i) -> p c t i", i=4),
+                z_grouped[hf][:, first * PACK : (first + count) * PACK].rearrange("p (c i t) -> p c t i", i=4, t=PACK),
+                z[:, :, start : start + count].rearrange("p t (c i) -> p c t i", i=4),
             )
 
+        share = 160
         finish_z(last, cols(1))
-        nc.scalar.activation(*weave(0), ACT.Copy)
-        nc.vector.tensor_copy(*weave(1))
+        nc.scalar.activation(*weave(0, 0, share), ACT.Copy)
+        nc.vector.tensor_copy(*weave(0, share, HALF - share))
+        nc.vector.tensor_copy(*weave(1, 0, HALF))
 
         h_acc = [psum.tile([P, S], F32, name="h_acc%d" % t, tag="bank%d" % (TILES + t)) for t in range(TILES)]
         h_sb = [keep.tile([P, 2 * S], F32, name="h_sb%d" % t, tag="h_sb%d" % t) for t in range(TILES)]
@@ -228,8 +254,8 @@ def tile_picked_twqpxbesh_none_p_kernel(
         for hf in range(2):
             quantize(z_q[0][:, cols(hf)], z_q[1][:, cols(hf)], z_grouped[hf][:])
         for t in range(TILES):
-            for hf in range(2):
-                product(h_acc[t][:, cols(hf)], dk, rows(t), z_q, cols(hf))
+            for span in [cols(0), cols(1)] if t == 0 else [slice(0, S)]:
+                product(h_acc[t][:, span], dk, rows(t), z_q, span)
 
         own = [keep.tile([P, S], F32, name="own%d" % t) for t in range(TILES)]
         ea2 = [keep.tile([P, S], F32, name="ea2_%d" % t) for t in range(TILES)]
@@ -254,7 +280,8 @@ def tile_picked_twqpxbesh_none_p_kernel(
         nc.gpsimd.memset(sixteenth[:], 0.0625)
         for t in range(TILES):
             inverse = keep.tile([P, S], F32, name="inverse%d" % t)
-            nc.scalar.activation(inverse[:], square[t][:], ACT.Abs_reciprocal_sqrt, bias=sixteenth[:], scale=1.0)
             result = keep.tile([P, S], F32, name="result%d" % t)
-            nc.vector.tensor_tensor(result[:], num[t][:], inverse[:], ALU.mult)
-            nc.sync.dma_start(out[rows(t), :], result[:])
+            for span in [slice(0, S)] if t < last else [cols(0), cols(1)]:
+                nc.scalar.activation(inverse[:, span], square[t][:, span], ACT.Abs_reciprocal_sqrt, bias=sixteenth[:], scale=1.0)
+                nc.vector.tensor_tensor(result[:, span], num[t][:, span], inverse[:, span], ALU.mult)
+                nc.sync.dma_start(out[rows(t), span], result[:, span])

@@ -42,9 +42,9 @@ def tile_picked_twqpxbesh_none_p_kernel(
         def cols(hf):
             return slice(hf * HALF, (hf + 1) * HALF)
 
-        def load_weight_half(name, w, hf):
-            raw = keep.tile([P, PACK, H // 2], F32, name=name)
-            nc.sync.dma_start(raw[:], w.rearrange("(p j) c -> p j c", j=PACK)[:, :, hf * (H // 2) : (hf + 1) * (H // 2)])
+        def load_weight(name, w, first, count):
+            raw = keep.tile([P, PACK, count], F32, name=name)
+            nc.sync.dma_start(raw[:], w.rearrange("(p j) c -> p j c", j=PACK)[:, :, first : first + count])
             return raw
 
         xs = keep.tile([P, T], U8, name="xs")
@@ -59,10 +59,10 @@ def tile_picked_twqpxbesh_none_p_kernel(
         nc.sync.dma_start(xw[:].bitcast(I32), x_words[0].rearrange("p n t -> p (n t)").bitcast(I32))
         for q in range(4):
             nc.sync.dma_start(xs[32 * q : 32 * q + 4, :].bitcast(I32), x_scales[0][4 * q : 4 * q + 4, :].bitcast(I32))
-        w1_raw = [load_weight_half("w1_raw%d" % hf, w1, hf) for hf in range(2)]
-        w2_raw = [load_weight_half("w2_raw0", w2, 0)]
+        w1_raw = load_weight("w1_raw", w1, 0, H)
+        w2_raw = [load_weight("w2_raw0", w2, 0, H // 2)]
         two_l = list_tile("two_l", two)
-        w2_raw.append(load_weight_half("w2_raw1", w2, 1))
+        w2_raw.append(load_weight("w2_raw1", w2, H // 2, H // 2))
         k1_l = list_tile("k1_l", k1)
         n2_l = list_tile("n2_l", n2)
         n1_l = list_tile("n1_l", n1)
@@ -94,19 +94,15 @@ def tile_picked_twqpxbesh_none_p_kernel(
             nc.vector.tensor_copy(picked[:], window[:].indirect(offsets[:]))
             return picked
 
-        def round_weight(name, raws, engines):
-            grouped = keep.tile([P, H * PACK], BF16, name=name, tag=name, align_bytes=64)
+        def round_weight(name, shares):
+            grouped = keep.tile([P, H * PACK], BF16, name=name, align_bytes=64)
             dealt = grouped[:].rearrange("p (t m j) -> p m t j", t=TILES, j=PACK)
-            for hf in range(2):
-                dst = dealt[:, hf * (P // 2) : (hf + 1) * (P // 2)]
-                src = raws[hf][:].rearrange("p j (m t) -> p m t j", t=TILES)
-                if engines[hf] == "vector":
-                    nc.vector.tensor_copy(dst, src)
-                elif engines[hf] == "gpsimd":
-                    nc.gpsimd.tensor_copy(dst, src)
-                else:
-                    nc.scalar.activation(dst, src, ACT.Copy)
+            for copy, raw, first_raw, first, count in shares:
+                copy(dealt[:, first : first + count], raw[:].rearrange("p j (m t) -> p m t j", t=TILES)[:, first_raw : first_raw + count])
             return grouped
+
+        def scalar_copy(dst, src):
+            nc.scalar.activation(dst, src, ACT.Copy)
 
         def quantize(codes, scales, values):
             nc.vector.quantize_mx(out=codes.bitcast(FP8X4), scales=scales, in_=values)
@@ -137,8 +133,8 @@ def tile_picked_twqpxbesh_none_p_kernel(
             return slice(t * P, (t + 1) * P)
 
         x_idx = (gather("x_idx_words", xw, offs_l, U32), gather("x_idx_scales", xs, offs_l, U8))
-        w1_grouped = round_weight("w1_grouped", w1_raw, ("scalar", "vector"))
-        w2_grouped = round_weight("w2_grouped", w2_raw, ("scalar", "gpsimd"))
+        w1_grouped = round_weight("w1_grouped", [(scalar_copy, w1_raw, 0, 0, 48), (nc.vector.tensor_copy, w1_raw, 48, 48, 80)])
+        w2_grouped = round_weight("w2_grouped", [(scalar_copy, w2_raw[0], 0, 0, 64), (nc.gpsimd.tensor_copy, w2_raw[1], 0, 64, 32), (nc.vector.tensor_copy, w2_raw[1], 32, 96, 32)])
         w1_q = quantize_weight("w1", w1_grouped)
         y_acc = []
         for t in range(TILES):

@@ -43,7 +43,7 @@ def tile_picked_twqpxbesh_none_p_kernel(
             return slice(hf * HALF, (hf + 1) * HALF)
 
         def load_weight(name, w, first, count):
-            raw = keep.tile([P, PACK, count], F32, name=name)
+            raw = keep.tile([P, PACK, count], F32, name=name, tag=name, align_bytes=64)
             nc.sync.dma_start(raw[:], w.rearrange("(p j) c -> p j c", j=PACK)[:, :, first : first + count])
             return raw
 
@@ -95,7 +95,7 @@ def tile_picked_twqpxbesh_none_p_kernel(
             return picked
 
         def round_weight(name, shares):
-            grouped = keep.tile([P, H * PACK], BF16, name=name, align_bytes=64)
+            grouped = keep.tile([P, H * PACK], BF16, name=name, tag=name, align_bytes=64)
             dealt = grouped[:].rearrange("p (t m j) -> p m t j", t=TILES, j=PACK)
             for copy, raw, first_raw, first, count in shares:
                 copy(dealt[:, first : first + count], raw[:].rearrange("p j (m t) -> p m t j", t=TILES)[:, first_raw : first_raw + count])
@@ -134,14 +134,14 @@ def tile_picked_twqpxbesh_none_p_kernel(
 
         x_idx = (gather("x_idx_words", xw, offs_l, U32), gather("x_idx_scales", xs, offs_l, U8))
         w1_grouped = round_weight("w1_grouped", [(scalar_copy, w1_raw, 0, 0, 48), (nc.vector.tensor_copy, w1_raw, 48, 48, 80)])
-        w2_grouped = round_weight("w2_grouped", [(scalar_copy, w2_raw[0], 0, 0, 64), (nc.gpsimd.tensor_copy, w2_raw[1], 0, 64, 32), (nc.vector.tensor_copy, w2_raw[1], 32, 96, 32)])
+        w2_grouped = round_weight("w2_grouped", [(scalar_copy, w2_raw[0], 0, 0, 64), (nc.gpsimd.tensor_copy, w2_raw[1], 0, 64, 64)])
         w1_q = quantize_weight("w1", w1_grouped)
         y_acc = []
         for t in range(TILES):
             acc = psum.tile([P, S], F32, name="y_acc%d" % t, tag="bank%d" % (TILES + t))
             product(acc[:], w1_q, rows(t), x_idx, slice(0, S))
             y_acc.append(acc)
-        x_two = (gather("x_two_words", xw, two_l, U32), gather("x_two_scales", xs, two_l, U8))
+        x_two = (gather("x_two_words", xw, two_l, U32, tag="w1_raw"), gather("x_two_scales", xs, two_l, U8, tag="w1_grouped"))
         w2_q = quantize_weight("w2", w2_grouped)
 
         y_far = keep.tile([P, TILES, S], F32, name="y_far")
@@ -199,8 +199,8 @@ def tile_picked_twqpxbesh_none_p_kernel(
         for hf in range(2):
             fetch_ea(last, cols(hf), half_list(n1_l, hf))
 
-        dk_picked = gather("dk_picked", ds, k1_l, U8, tag="x_two_words")
-        dk_words = gather("dk_words", dw, k1_l, U32)
+        dk_picked = gather("dk_picked", ds, k1_l, U8, tag="w1_raw")
+        dk_words = gather("dk_words", dw, k1_l, U32, tag="w1_grouped")
         for r in range(4):
             src = 16 * (r // 2) + r % 2
             nc.sync.dma_start(dk_scales[r:P:32, :].bitcast(I32), dk_picked[src:P:32, :].bitcast(I32))

from contextlib import ExitStack

import concourse.mybir as mybir

K, T, S, H, G = 512, 1024, 512, 512, 2048
FLOPS = 3 * 2 * K * H * S

F32 = mybir.dt.float32
BF16 = mybir.dt.bfloat16
I32 = mybir.dt.int32
U32 = mybir.dt.uint32
U16 = mybir.dt.uint16
U8 = mybir.dt.uint8
FP8X4 = mybir.dt.float8_e4m3fn_x4
ALU = mybir.AluOpType
ACT = mybir.ActivationFunctionType

P = 128
PACK = 4
TILES = H // P
HALF = S // 2
LIST_COLS = S // 16


def tile_picked_twqpxbesh_none_p_kernel(
    tc, x_words, x_scales, w1, w2, tau, gs, d_words, d_scales, tau2, offs, two, n1, n2, k1, n3, out
):
    nc = tc.nc
    with ExitStack() as ctx:
        lists = ctx.enter_context(tc.tile_pool(name="lists", bufs=1))
        keep = ctx.enter_context(tc.tile_pool(name="keep", bufs=1))
        psum = ctx.enter_context(tc.psum_pool(name="psum", bufs=1))

        def list_tile(name, src):
            tile = lists.tile([P, LIST_COLS], U16, name=name)
            nc.sync.dma_start(tile[:], src)
            return tile

        def half_list(tile, hf):
            return tile[:, hf * (LIST_COLS // 2) : (hf + 1) * (LIST_COLS // 2)]

        def cols(hf):
            return slice(hf * HALF, (hf + 1) * HALF)

        def load_weight(name, w, first, count):
            raw = keep.tile([P, PACK, count], F32, name=name, tag=name, align_bytes=64)
            nc.sync.dma_start(raw[:], w.rearrange("(p j) c -> p j c", j=PACK)[:, :, first : first + count])
            return raw

        xs = keep.tile([P, T], U8, name="xs")
        nc.gpsimd.memset(xs[:].bitcast(I32), 0)
        ds = keep.tile([P, G], U8, name="ds")
        nc.gpsimd.memset(ds[:].bitcast(I32), 0)
        dk_scales = keep.tile([P, H], U8, name="dk_scales", align_bytes=64)
        nc.gpsimd.memset(dk_scales[:].bitcast(I32), 0)

        offs_l = list_tile("offs_l", offs)
        xw = keep.tile([P, T], U32, name="xw")
        nc.sync.dma_start(xw[:].bitcast(I32), x_words[0].rearrange("p n t -> p (n t)").bitcast(I32))
        for q in range(4):
            nc.sync.dma_start(xs[32 * q : 32 * q + 4, :].bitcast(I32), x_scales[0][4 * q : 4 * q + 4, :].bitcast(I32))
        w1_raw = load_weight("w1_raw", w1, 0, H)
        w2_raw = [load_weight("w2_raw0", w2, 0, H // 2)]
        two_l = list_tile("two_l", two)
        w2_raw.append(load_weight("w2_raw1", w2, H // 2, H // 2))
        k1_l = list_tile("k1_l", k1)
        n2_l = list_tile("n2_l", n2)
        n1_l = list_tile("n1_l", n1)
        dw = keep.tile([P, G], U32, name="dw")
        nc.sync.dma_start(dw[:].bitcast(I32), d_words[0].rearrange("p n t -> p (n t)").bitcast(I32))
        n3_l = list_tile("n3_l", n3)

        tau2_t = keep.tile([P, TILES], F32, name="tau2_t")
        with nc.allow_non_contiguous_dma(reason="one value a partition and tile"):
            nc.sync.dma_start(tau2_t[:], tau2.rearrange("(t p) o -> p (t o)", p=P))

        tau_t = keep.tile([P, TILES], F32, name="tau_t")
        nc.gpsimd.dma_start(tau_t[:], tau.rearrange("(p t) o -> p (t o)", t=TILES))
        gs_t = keep.tile([P, TILES], F32, name="gs_t")
        nc.gpsimd.dma_start(gs_t[:], gs.rearrange("(p t) o -> p (t o)", t=TILES))
        for r in range(2):
            nc.gpsimd.dma_start(
                ds[r:P:16, :].bitcast(I32), d_scales[0].rearrange("(g r) c -> r g c", r=2)[r].bitcast(I32)
            )
        gs_twice = keep.tile([P, TILES], F32, name="gs_twice")
        nc.gpsimd.tensor_scalar(gs_twice[:], gs_t[:], 2.0, 0.0, ALU.mult, ALU.add)
        tau_neg = keep.tile([P, TILES], F32, name="tau_neg")
        nc.gpsimd.tensor_scalar(tau_neg[:], tau_t[:], -1.0, 0.0, ALU.mult, ALU.add)
        gs_neg_half = keep.tile([P, TILES], F32, name="gs_neg_half")
        nc.gpsimd.tensor_scalar(gs_neg_half[:], gs_t[:], -0.5, 0.0, ALU.mult, ALU.add)

        def gather(name, window, offsets, dtype, tag=None):
            picked = keep.tile([P, S], dtype, name=name, tag=tag or name, align_bytes=64)
            nc.vector.tensor_copy(picked[:], window[:].indirect(offsets[:]))
            return picked

        def round_weight(name, shares):
            grouped = keep.tile([P, H * PACK], BF16, name=name, tag=name, align_bytes=64)
            dealt = grouped[:].rearrange("p (t m j) -> p m t j", t=TILES, j=PACK)
            for copy, raw, first_raw, first, count in shares:
                copy(dealt[:, first : first + count], raw[:].rearrange("p j (m t) -> p m t j", t=TILES)[:, first_raw : first_raw + count])
            return grouped

        def scalar_copy(dst, src):
            nc.scalar.activation(dst, src, ACT.Copy)

        def quantize(codes, scales, values):
            nc.vector.quantize_mx(out=codes.bitcast(FP8X4), scales=scales, in_=values)

        def mx_tiles(name):
            codes = keep.tile([P, H], U32, name=name + "_codes", tag=name + "_codes", align_bytes=64)
            scales = keep.tile([P, H], U8, name=name + "_scales", tag=name + "_scales", align_bytes=64)
            return codes, scales

        def quantize_weight(name, grouped):
            codes, scales = mx_tiles(name)
            quantize(codes[:, :P], scales[:, :P], grouped[:, : P * PACK])
            quantize(codes[:, P:], scales[:, P:], grouped[:, P * PACK :])
            return codes, scales

        def product(acc, lhs, lhs_cols, rhs, rhs_cols):
            nc.tensor.matmul_mx(
                out=acc,
                lhsT=lhs[0][:, lhs_cols].bitcast(FP8X4),
                lhsT_scale=lhs[1][:, lhs_cols],
                rhs=rhs[0][:, rhs_cols].bitcast(FP8X4),
                rhs_scale=rhs[1][:, rhs_cols],
                start=True,
                stop=True,
            )

        def rows(t):
            return slice(t * P, (t + 1) * P)

        x_idx = (gather("x_idx_words", xw, offs_l, U32), gather("x_idx_scales", xs, offs_l, U8))
        w1_grouped = round_weight("w1_grouped", [(scalar_copy, w1_raw, 0, 0, 48), (nc.vector.tensor_copy, w1_raw, 48, 48, 80)])
        w2_grouped = round_weight("w2_grouped", [(scalar_copy, w2_raw[0], 0, 0, 64), (nc.gpsimd.tensor_copy, w2_raw[1], 0, 64, 64)])
        w1_q = quantize_weight("w1", w1_grouped)
        y_acc = []
        for t in range(TILES):
            acc = psum.tile([P, S], F32, name="y_acc%d" % t, tag="bank%d" % (TILES + t))
            product(acc[:], w1_q, rows(t), x_idx, slice(0, S))
            y_acc.append(acc)
        x_two = (gather("x_two_words", xw, two_l, U32, tag="w1_raw"), gather("x_two_scales", xs, two_l, U8, tag="w1_grouped"))
        w2_q = quantize_weight("w2", w2_grouped)

        y_far = keep.tile([P, TILES, S], F32, name="y_far")
        diff = keep.tile([P, 2, S], F32, name="diff")
        prod = keep.tile([P, 2, S], F32, name="prod")
        z = keep.tile([P, TILES, S], F32, name="z")

        top = keep.tile([P, TILES], F32, name="top")
        bias1 = [keep.tile([P, 1], F32, name="bias1_%d" % t) for t in range(TILES)]
        d_sb = []
        d_acc = []
        for t in range(TILES):
            acc = psum.tile([P, S], F32, name="d_acc%d" % t, tag="bank%d" % t)
            product(acc[:], w2_q, rows(t), x_two, slice(0, S))
            window = keep.tile([P, 2 * S], F32, name="d_sb%d" % t, tag="d_sb%d" % t)
            nc.vector.tensor_scalar(window[:, :S], acc[:], 1.0, None, ALU.mult, ALU.max, accum_out=top[:, t : t + 1])
            if t < 2:
                nc.scalar.activation(bias1[t][:], top[:, t : t + 1], ACT.Copy, scale=tau_neg[:, t : t + 1])
            else:
                nc.gpsimd.tensor_tensor(bias1[t][:], top[:, t : t + 1], tau_neg[:, t : t + 1], ALU.mult)
            d_sb.append(window)
            d_acc.append(acc)

        last = TILES - 1

        y_sb = []

        def ea(t, span):
            return y_sb[t][:, S + span.start : S + span.stop]

        def diff_of(t, span):
            return ea(1, span) if t == last else diff[:, min(t, 1), span]

        def difference(t):
            nc.gpsimd.tensor_tensor(diff_of(t, slice(0, S)), y_sb[t][:, :S], y_far[:, t, :], ALU.subtract)

        def fetch_ea(t, span, offsets):
            nc.scalar.activation(
                ea(t, span), d_sb[t][:].indirect(offsets), ACT.Exp, bias=bias1[t][:], scale=tau_t[:, t : t + 1]
            )

        for t in range(TILES):
            if t < 2:
                window = keep.tile([P, 2 * S], F32, name="y_sb%d" % t)
                nc.scalar.activation(window[:, :S], y_acc[t][:], ACT.Copy, scale=gs_twice[:, t : t + 1])
            else:
                window = keep.tile([P, 2 * S], F32, name="y_sb%d" % t, tag=("w2_codes", "w2_scales")[t - 2], align_bytes=64)
                nc.vector.tensor_scalar(window[:, :S], y_acc[t][:], gs_twice[:, t : t + 1], None, ALU.mult)
            y_sb.append(window)
            nc.scalar.activation(y_far[:, t, :], window[:].indirect(n2_l[:]), ACT.Copy)
            if t < 2:
                difference(t)
            if t < last:
                fetch_ea(t, slice(0, S), n1_l[:])
        for hf in range(2):
            fetch_ea(last, cols(hf), half_list(n1_l, hf))

        dk_picked = gather("dk_picked", ds, k1_l, U8, tag="w1_raw")
        dk_words = gather("dk_words", dw, k1_l, U32, tag="w1_grouped")
        for r in range(4):
            src = 16 * (r // 2) + r % 2
            nc.sync.dma_start(dk_scales[r:P:32, :].bitcast(I32), dk_picked[src:P:32, :].bitcast(I32))
        dk = (dk_words, dk_scales)

        slots = (0, 1, 1, 0)

        def multiply(engine, t, span):
            engine.tensor_tensor(prod[:, slots[t], span], ea(t, span), diff_of(t, span), ALU.mult)

        def finish_z(t, span):
            nc.vector.scalar_tensor_tensor(
                z[:, t, span], d_acc[t][:, span], gs_neg_half[:, t : t + 1], prod[:, slots[t], span], ALU.mult, ALU.add
            )

        for t in range(2):
            multiply(nc.gpsimd, t, slice(0, S))
            finish_z(t, slice(0, S))
        difference(2)
        difference(last)
        multiply(nc.vector, 2, slice(0, S))
        multiply(nc.vector, last, cols(0))
        finish_z(2, slice(0, S))
        multiply(nc.vector, last, cols(1))
        finish_z(last, cols(0))

        z_q = mx_tiles("z")
        z_grouped = [keep.tile([P, HALF * PACK], BF16, name="z_grouped%d" % hf, align_bytes=64) for hf in range(2)]

        def weave(hf, first, count):
            start = hf * HALF + first
            return (
                z_grouped[hf][:, first * PACK : (first + count) * PACK].rearrange("p (c i t) -> p c t i", i=4, t=PACK),
                z[:, :, start : start + count].rearrange("p t (c i) -> p c t i", i=4),
            )

        share = 160
        finish_z(last, cols(1))
        nc.scalar.activation(*weave(0, 0, share), ACT.Copy)
        nc.vector.tensor_copy(*weave(0, share, HALF - share))
        nc.vector.tensor_copy(*weave(1, 0, HALF))

        h_acc = [psum.tile([P, S], F32, name="h_acc%d" % t, tag="bank%d" % (TILES + t)) for t in range(TILES)]
        h_sb = [keep.tile([P, 2 * S], F32, name="h_sb%d" % t, tag="h_sb%d" % t) for t in range(TILES)]
        top2 = keep.tile([P, TILES], F32, name="top2")
        bias2 = keep.tile([P, TILES], F32, name="bias2")
        for hf in range(2):
            quantize(z_q[0][:, cols(hf)], z_q[1][:, cols(hf)], z_grouped[hf][:])
        for t in range(TILES):
            for span in [cols(0), cols(1)] if t == 0 else [slice(0, S)]:
                product(h_acc[t][:, span], dk, rows(t), z_q, span)

        own = [keep.tile([P, S], F32, name="own%d" % t) for t in range(TILES)]
        ea2 = [keep.tile([P, S], F32, name="ea2_%d" % t) for t in range(TILES)]
        num = [keep.tile([P, S], F32, name="num%d" % t) for t in range(TILES)]
        both = [keep.tile([P, S], F32, name="both%d" % t) for t in range(TILES)]
        square = [keep.tile([P, S], F32, name="square%d" % t) for t in range(TILES)]
        for t in range(TILES):
            nc.vector.tensor_scalar(
                h_sb[t][:, :S], h_acc[t][:], 0.0625, None, ALU.mult, ALU.max, accum_out=top2[:, t : t + 1]
            )
            nc.gpsimd.tensor_scalar(bias2[:, t : t + 1], top2[:, t : t + 1], tau2_t[:, t : t + 1], -1.0, ALU.mult, ALU.mult)
        for t in range(TILES):
            nc.scalar.activation(own[t][:], h_sb[t][:, :S], ACT.Exp, bias=bias2[:, t : t + 1], scale=tau2_t[:, t : t + 1])
            nc.scalar.activation(
                ea2[t][:], h_sb[t][:].indirect(n3_l[:]), ACT.Exp, bias=bias2[:, t : t + 1], scale=tau2_t[:, t : t + 1]
            )
            nc.vector.scalar_tensor_tensor(num[t][:], h_acc[t][:], 0.125, own[t][:], ALU.mult, ALU.mult)
            nc.vector.tensor_tensor(both[t][:], own[t][:], ea2[t][:], ALU.add)
            nc.vector.scalar_tensor_tensor(square[t][:], both[t][:], 0.5, both[t][:], ALU.add, ALU.mult)

        sixteenth = keep.tile([P, 1], F32, name="sixteenth", tag="h_sb%d" % last)
        nc.gpsimd.memset(sixteenth[:], 0.0625)
        for t in range(TILES):
            inverse = keep.tile([P, S], F32, name="inverse%d" % t)
            result = keep.tile([P, S], F32, name="result%d" % t)
            for span in [slice(0, S)] if t < last else [cols(0), cols(1)]:
                nc.scalar.activation(inverse[:, span], square[t][:, span], ACT.Abs_reciprocal_sqrt, bias=sixteenth[:], scale=1.0)
                nc.vector.tensor_tensor(result[:, span], num[t][:, span], inverse[:, span], ALU.mult)
                nc.sync.dma_start(out[rows(t), span], result[:, span])
